import numpy as np
import ml_dtypes


def mxq(x, axis, fmt="e4m3"):
    dtype, down = {"e4m3": (ml_dtypes.float8_e4m3fn, 7), "e5m2": (ml_dtypes.float8_e5m2, 14)}[fmt]
    v = np.moveaxis(np.asarray(x, np.float32).astype(ml_dtypes.bfloat16).astype(np.float64), axis, -1)
    blocks = v.reshape(v.shape[:-1] + (-1, 32))
    amax = np.abs(blocks).max(-1, keepdims=True)
    byte = np.maximum(np.where(amax > 0, np.frexp(amax)[1] - 1 + 127, 0) - down, 1)
    scale = np.exp2(byte - 127.0)
    codes = (blocks / scale).astype(np.float32).astype(dtype).astype(np.float64)
    return np.moveaxis((codes * scale).reshape(v.shape), -1, axis)


WIDE = False


def mx_kscale(k):
    if not WIDE:
        return np.ones(k)
    levels = np.array([10, -10, 5, -5, 0])
    if k % 512:
        return np.exp2(np.random.permutation(np.resize(levels, k // 32))).repeat(32)
    a = np.empty((k // 512, 16))
    for p in range(k // 512):
        a[p, :8] = np.random.permutation(np.resize(levels, 8))
        for g in range(8):
            far = levels[np.abs(levels - a[p, g]) >= 10]
            a[p, g + 8] = far[np.random.randint(len(far))]
    return np.exp2(a.ravel()).repeat(32)


def f64(x):
    return np.asarray(x).astype(np.float64)


def striped(idx):
    return np.tile(idx.reshape(-1, 16).T, (8, 1)).astype(np.uint16)


def unstriped(offs):
    return offs[:16].T.reshape(-1).astype(np.int64)


E2M1 = np.array([0.0, 0.5, 1.0, 1.5, 2.0, 3.0, 4.0, 6.0, -0.0, -0.5, -1.0, -1.5, -2.0, -3.0, -4.0, -6.0])


def pack_weight(w, fmt):
    k, n = w.shape
    w = f64(np.asarray(w, np.float32).astype(ml_dtypes.bfloat16)).reshape(k // 32, 32, n)
    amax = np.abs(w).max(1)
    if fmt == "e4m3":
        byte = np.frexp(amax)[1] - 1 + 127 - 7
    else:
        mant, ex = np.frexp(amax / 6.0)
        byte = np.where(mant > 0.5, ex, ex - 1) + 127
    byte = np.clip(np.where(amax > 0, byte, 1), 1, 254)
    scaled = (w * np.exp2(127.0 - byte)[:, None, :]).reshape(k, n).astype(np.float32)
    by_word = np.ascontiguousarray(scaled.reshape(k // 512, 128, 4, n).transpose(0, 1, 3, 2))
    if fmt == "e4m3":
        words = by_word.astype(ml_dtypes.float8_e4m3fn).view(np.uint8)
    else:
        c = by_word.astype(ml_dtypes.float4_e2m1fn).view(np.uint8) & 0xF
        words = (c[..., 0::2] | (c[..., 1::2] << 4)).reshape(k // 512, 128, 2 * n)
    return np.ascontiguousarray(words), np.ascontiguousarray(byte.astype(np.uint8).reshape(k // 512, 16, n))


def unpack_weight(words, scales, fmt):
    g, _, n = scales.shape
    words = np.ascontiguousarray(words).reshape(g, 128, n, -1)
    if fmt == "e4m3":
        vals = words.view(ml_dtypes.float8_e4m3fn).astype(np.float64)
    else:
        nib = np.empty((g, 128, n, 4), np.uint8)
        nib[..., 0::2] = words & 0xF
        nib[..., 1::2] = words >> 4
        vals = E2M1[nib]
    vals = vals * np.repeat(np.exp2(scales.astype(np.float64) - 127.0), 8, axis=1)[..., None]
    return vals.transpose(0, 1, 3, 2).reshape(g * 512, n)


def planes(y):
    n, m = y.shape
    v = y.astype(np.float32).astype(ml_dtypes.bfloat16).astype(np.float64).reshape(n // 32, 32, m)
    top = np.abs(v).max(1)
    byte = np.clip(np.where(top > 0, np.frexp(top)[1] - 1 + 127 - 7, 1), 1, 254)
    codes = (v * np.exp2(127.0 - byte)[:, None, :]).reshape(n, m).astype(np.float32).astype(ml_dtypes.float8_e4m3fn).view(np.uint8)
    words = codes.reshape(n // 512, 128, 4, m).transpose(0, 1, 3, 2)
    return np.ascontiguousarray(words), np.ascontiguousarray(byte.astype(np.uint8).reshape(n // 512, 16, m))


def relu(v):
    return np.maximum(v, 0.0)


K, T, E, C, H, N = 512, 512, 2, 256, 512, 512


def by_expert(wq, xq):
    return np.concatenate([wq[e].T @ xq[:, e * C:(e + 1) * C] for e in range(E)], axis=1)


def setup_inputs():
    n = np.random.standard_normal
    s = mx_kscale(K)
    u = mx_kscale(H)
    slot_token = np.random.permutation(T)[:E * C]
    partner = np.concatenate([np.random.permutation(T) for _ in range(-(-E * C // T))])[:E * C]
    x = pack_weight(n((K, T)) * s[:, None], "e4m3")
    wp = [pack_weight(m, "e2m1") for m in n((E, K, H)) / np.sqrt(K) / s[None, :, None] * u]
    return {
        "x_words": x[0],
        "x_scales": x[1],
        "w1": (n((E, K, H)) / np.sqrt(K) / s[None, :, None] * u).astype(np.float32),
        "wp_words": np.stack([m[0] for m in wp]),
        "wp_scales": np.stack([m[1] for m in wp]),
        "w2": (n((E, H, N)) / np.sqrt(H) / u[None, :, None]).astype(np.float32),
        "gate": np.tile(np.random.uniform(0.2, 1.0, E * C), (128, 1)).astype(np.float32),
        "offs": striped(slot_token),
        "offs2": striped(partner),
    }


def reference(x_words, x_scales, w1, wp_words, wp_scales, w2, gate, offs, offs2):
    w1q = mxq(f64(w1), 1, "e4m3")
    wp = np.stack([unpack_weight(wp_words[e], wp_scales[e], "e2m1") for e in range(E)])
    w2q = mxq(f64(w2), 1, "e4m3")
    idx, idx2 = unstriped(offs), unstriped(offs2)
    x = unpack_weight(x_words, x_scales, "e4m3")
    h = relu(by_expert(w1q, x[:, idx]) + by_expert(wp, x[:, idx2]))
    y = by_expert(w2q, mxq(h, 0, "e4m3"))
    out = np.zeros((N, T))
    out[:, idx] = f64(gate[:1]) * y
    out_0 = out
    return (out_0,) + planes(out_0)

@@ -1,0 +1,263 @@
+from contextlib import ExitStack
+
+import concourse.mybir as mybir
+
+K, T, E, C, H, N = 512, 512, 2, 256, 512, 512
+FLOPS = 2 * E * C * (2 * K * H + H * N)
+
+F32 = mybir.dt.float32
+BF16 = mybir.dt.bfloat16
+I32 = mybir.dt.int32
+U32 = mybir.dt.uint32
+U16 = mybir.dt.uint16
+U8 = mybir.dt.uint8
+FP8X4 = mybir.dt.float8_e4m3fn_x4
+FP4X4 = mybir.dt.float4_e2m1fn_x4
+MULT = mybir.AluOpType.mult
+ADD = mybir.AluOpType.add
+RELU = mybir.ActivationFunctionType.Relu
+COPY = mybir.ActivationFunctionType.Copy
+
+P = 128
+PACK = 4
+HALF = 256
+LIST_COLS = C // 16
+
+
+def tile_moe_duo_relu_kernel(
+    tc, x_words, x_scales, w1, wp_words, wp_scales, w2, gate, offs, offs2, out_0, out_1, out_2
+):
+    nc = tc.nc
+    with ExitStack() as ctx:
+        sb = ctx.enter_context(tc.tile_pool(name="sb", bufs=1))
+        ps = ctx.enter_context(tc.psum_pool(name="ps", bufs=1))
+
+        def tile(shape, dtype, name):
+            return sb.tile(shape, dtype, name=name, align_bytes=64)
+
+        tok_list = sb.tile([P, T // 16], U16, name="tok_list")
+        par_list = sb.tile([P, T // 16], U16, name="par_list")
+        xw = tile([P, T], I32, "xw")
+        xs = tile([P, T], U8, "xs")
+        wpw = tile([P, E, 2 * H], U8, "wpw")
+        wps = tile([P, E, H], U8, "wps")
+        gate_sb = tile([P, E * C], F32, "gate_sb")
+
+        nc.gpsimd.memset(xs[:].bitcast(I32), 0)
+        nc.gpsimd.memset(wps[:].rearrange("p e i -> p (e i)").bitcast(I32), 0)
+
+        raw = {}
+
+        def load_weight_half(name, w, e, half):
+            raw[name, e, half] = tile([P, PACK, HALF], F32, "raw_%s_%d_%d" % (name, e, half))
+            rows = w[e].rearrange("(p j) c -> p j c", j=PACK)
+            nc.sync.dma_start(out=raw[name, e, half][:], in_=rows[:, :, half * HALF : (half + 1) * HALF])
+
+        nc.sync.dma_start(tok_list[:], offs)
+        nc.sync.dma_start(out=xw[:], in_=x_words[0].rearrange("p t d -> p (t d)").bitcast(I32))
+        load_weight_half("w1", w1, 0, 0)
+        nc.sync.dma_start(par_list[:], offs2)
+        xs_rows = x_scales[0].bitcast(I32)
+        for r in range(4):
+            nc.sync.dma_start(out=xs[:].bitcast(I32)[r:P:32, :], in_=xs_rows[r:16:4, :])
+        load_weight_half("w1", w1, 0, 1)
+        nc.sync.dma_start(
+            out=wpw[:].bitcast(I32), in_=wp_words.rearrange("e s p b -> p (e s) b").bitcast(I32)
+        )
+        wps_rows = wp_scales.rearrange("e s b i -> b (e s) i").bitcast(I32)
+        for r in range(4):
+            nc.sync.dma_start(out=wps[:].bitcast(I32)[r:P:32, :, :], in_=wps_rows[r:16:4, :, :])
+        load_weight_half("w1", w1, 1, 0)
+        load_weight_half("w1", w1, 1, 1)
+        load_weight_half("w2", w2, 0, 0)
+        load_weight_half("w2", w2, 0, 1)
+        nc.sync.dma_start(out=gate_sb[:], in_=gate)
+        load_weight_half("w2", w2, 1, 0)
+        load_weight_half("w2", w2, 1, 1)
+
+        gathered = {}
+
+        def gather(e):
+            cols = slice(e * LIST_COLS, (e + 1) * LIST_COLS)
+            for name, lst in (("tok", tok_list), ("par", par_list)):
+                words = tile([P, C], U32, "%s_words_%d" % (name, e))
+                nc.vector.tensor_copy(out=words[:], in_=xw[:].bitcast(U32).indirect(lst[:, cols]))
+                gathered[name, "words", e] = words
+            for name, lst in (("par", par_list), ("tok", tok_list)):
+                scales = tile([P, C], U8, "%s_scales_%d" % (name, e))
+                nc.vector.tensor_copy(out=scales[:], in_=xs[:].indirect(lst[:, cols]))
+                gathered[name, "scales", e] = scales
+
+        dealt = {}
+
+        def deal_wp(e):
+            words = tile([P, 2 * H], U8, "wp_dealt_words_%d" % e)
+            nc.scalar.copy(
+                out=words[:].bitcast(U16).rearrange("p (t m) -> p m t", t=PACK),
+                in_=wpw[:, e, :].bitcast(U16).rearrange("p (m t) -> p m t", t=PACK),
+            )
+            scales = tile([P, H], U8, "wp_dealt_scales_%d" % e)
+            nc.vector.tensor_copy(
+                out=scales[:].rearrange("p (t m) -> p m t", t=PACK),
+                in_=wps[:, e, :].rearrange("p (m t) -> p m t", t=PACK),
+            )
+            dealt[e] = (words, scales)
+
+        def round_on(engine, out, in_):
+            if engine == "gpsimd":
+                nc.gpsimd.tensor_scalar(out, in_, 1.0, 0.0, MULT, ADD)
+            elif engine == "scalar":
+                nc.scalar.copy(out=out, in_=in_)
+            else:
+                nc.vector.tensor_copy(out=out, in_=in_)
+
+        rounded = {}
+        quantised = {}
+
+        def round_weight(name, e, engines):
+            for pair in range(2):
+                rounded[name, e, pair] = tile([P, 2, P, PACK], BF16, "rounded_%s_%d_%d" % (name, e, pair))
+            for half in range(2):
+                src = raw[name, e, half][:].rearrange("p j (m t) -> p m j t", t=PACK)
+                for pair in range(2):
+                    dst = rounded[name, e, pair][:].rearrange("p t m j -> p m j t")
+                    round_on(
+                        engines[pair],
+                        dst[:, half * 64 : (half + 1) * 64, :, :],
+                        src[:, :, :, 2 * pair : 2 * pair + 2],
+                    )
+
+        def quantise_weight(name, e):
+            for pair in range(2):
+                codes = tile([P, 2 * P], U32, "codes_%s_%d_%d" % (name, e, pair))
+                scales = tile([P, 2 * P], U8, "scales_%s_%d_%d" % (name, e, pair))
+                nc.vector.quantize_mx(
+                    out=codes[:].bitcast(FP8X4),
+                    scales=scales[:],
+                    in_=rounded[name, e, pair][:].rearrange("p t m j -> p (t m j)"),
+                )
+                quantised[name, e, pair] = (codes, scales)
+
+        h_banks = {}
+
+        def partner_products(e):
+            words, scales = dealt[e]
+            for s in range(2):
+                bank = ps.tile([P, PACK, P], F32, name="h_bank_%d_%d" % (e, s))
+                h_banks[e, s] = bank
+                slots = slice(s * P, (s + 1) * P)
+                for t in range(PACK):
+                    nc.tensor.matmul_mx(
+                        out=bank[:, t, :],
+                        lhsT=words[:, 2 * P * t : 2 * P * (t + 1)].bitcast(FP4X4),
+                        lhsT_scale=scales[:, P * t : P * (t + 1)],
+                        rhs=gathered["par", "words", e][:, slots].bitcast(FP8X4),
+                        rhs_scale=gathered["par", "scales", e][:, slots],
+                        start=(t == 0),
+                        stop=False,
+                    )
+
+        hq = {}
+
+        def first_layer(e):
+            h_rounded = tile([P, C, PACK], BF16, "h_rounded_%d" % e)
+            for s in range(2):
+                bank = h_banks[e, s]
+                slots = slice(s * P, (s + 1) * P)
+                for t in range(PACK):
+                    codes, scales = quantised["w1", e, t // 2]
+                    cols = slice((t % 2) * P, (t % 2 + 1) * P)
+                    nc.tensor.matmul_mx(
+                        out=bank[:, t, :],
+                        lhsT=codes[:, cols].bitcast(FP8X4),
+                        lhsT_scale=scales[:, cols],
+                        rhs=gathered["tok", "words", e][:, slots].bitcast(FP8X4),
+                        rhs_scale=gathered["tok", "scales", e][:, slots],
+                        start=False,
+                        stop=(t == PACK - 1),
+                    )
+                nc.scalar.activation(
+                    out=h_rounded[:, slots, :], in_=bank[:].rearrange("p t n -> p n t"), func=RELU
+                )
+            codes = tile([P, C], U32, "h_codes_%d" % e)
+            scales = tile([P, C], U8, "h_scales_%d" % e)
+            nc.vector.quantize_mx(
+                out=codes[:].bitcast(FP8X4), scales=scales[:], in_=h_rounded[:].rearrange("p n t -> p (n t)")
+            )
+            hq[e] = (codes, scales)
+
+        result = [tile([P, T], F32, "result_%d" % t) for t in range(PACK)]
+
+        def second_layer(e, scalar_tiles):
+            h_codes, h_scales = hq[e]
+            cols = slice(e * LIST_COLS, (e + 1) * LIST_COLS)
+            gated = {}
+            for pair in range(2):
+                codes, scales = quantised["w2", e, pair]
+                bank = ps.tile([P, 2, C], F32, name="y_bank_%d_%d" % (e, pair))
+                for u in range(2):
+                    nc.tensor.matmul_mx(
+                        out=bank[:, u, :],
+                        lhsT=codes[:, u * P : (u + 1) * P].bitcast(FP8X4),
+                        lhsT_scale=scales[:, u * P : (u + 1) * P],
+                        rhs=h_codes[:].bitcast(FP8X4),
+                        rhs_scale=h_scales[:],
+                        start=True,
+                        stop=True,
+                    )
+                gated[pair] = tile([P, 2, C], F32, "gated_%d_%d" % (e, pair))
+                nc.vector.tensor_tensor(
+                    gated[pair][:],
+                    bank[:],
+                    gate_sb[:, e * C : (e + 1) * C].unsqueeze(1).to_broadcast([P, 2, C]),
+                    MULT,
+                )
+            for t in range(PACK):
+                window = result[t][:].indirect(tok_list[:, cols])
+                values = gated[t // 2][:, t % 2, :]
+                if t < scalar_tiles:
+                    nc.scalar.activation(window, values, COPY)
+                else:
+                    nc.vector.tensor_copy(window, values)
+
+        gather(0)
+        gather(1)
+        deal_wp(0)
+        deal_wp(1)
+        round_weight("w1", 0, ("scalar", "scalar"))
+        round_weight("w1", 1, ("scalar", "scalar"))
+        partner_products(0)
+        partner_products(1)
+        quantise_weight("w1", 0)
+        first_layer(0)
+        quantise_weight("w1", 1)
+        first_layer(1)
+        round_weight("w2", 0, ("vector", "vector"))
+        quantise_weight("w2", 0)
+        second_layer(0, 4)
+        round_weight("w2", 1, ("vector", "vector"))
+        quantise_weight("w2", 1)
+        second_layer(1, 1)
+
+        out_rows = out_0.rearrange("(p t) c -> p t c", t=PACK)
+        planes = tile([P, PACK, T], BF16, "planes")
+        for t, engine in ((0, "scalar"), (1, "scalar"), (2, "scalar"), (3, "vector")):
+            nc.sync.dma_start(out=out_rows[:, t, :], in_=result[t][:])
+            round_on(engine, planes[:, t, :], result[t][:])
+        woven = tile([P, T, PACK], BF16, "woven")
+        src = planes[:].rearrange("p t (c i) -> p c t i", i=4)
+        dst = woven[:].rearrange("p (c i) t -> p c t i", i=4)
+        nc.vector.tensor_copy(out=dst[:, :96], in_=src[:, :96])
+        nc.scalar.copy(out=dst[:, 96:], in_=src[:, 96:])
+        out_codes = tile([P, T], I32, "out_codes")
+        out_scales = tile([P, T], U8, "out_scales")
+        nc.vector.quantize_mx(
+            out=out_codes[:].bitcast(FP8X4), scales=out_scales[:], in_=woven[:].rearrange("p c t -> p (c t)")
+        )
+        nc.sync.dma_start(out=out_1[0].rearrange("p t d -> p (t d)").bitcast(I32), in_=out_codes[:])
+        scale_rows = out_2[0].bitcast(I32)
+        for q in range(4):
+            queue = nc.scalar if q % 2 else nc.sync
+            queue.dma_start(
+                out=scale_rows[4 * q : 4 * q + 4, :], in_=out_scales[:].bitcast(I32)[32 * q : 32 * q + 4, :]
+            )

@@ -32,8 +32,8 @@ def tile_moe_duo_relu_kernel(
         sb = ctx.enter_context(tc.tile_pool(name="sb", bufs=1))
         ps = ctx.enter_context(tc.psum_pool(name="ps", bufs=1))
 
-        def tile(shape, dtype, name):
-            return sb.tile(shape, dtype, name=name, align_bytes=64)
+        def tile(shape, dtype, name, tag=None):
+            return sb.tile(shape, dtype, name=name, tag=tag or name, align_bytes=64)
 
         tok_list = sb.tile([P, T // 16], U16, name="tok_list")
         par_list = sb.tile([P, T // 16], U16, name="par_list")
@@ -48,65 +48,52 @@ def tile_moe_duo_relu_kernel(
 
         raw = {}
 
-        def load_weight_half(name, w, e, half):
-            raw[name, e, half] = tile([P, PACK, HALF], F32, "raw_%s_%d_%d" % (name, e, half))
+        def load_weight(name, w, e, first, last):
+            raw[name, e, first] = tile([P, PACK, last - first], F32, "raw_%s_%d_%d" % (name, e, first))
             rows = w[e].rearrange("(p j) c -> p j c", j=PACK)
-            nc.sync.dma_start(out=raw[name, e, half][:], in_=rows[:, :, half * HALF : (half + 1) * HALF])
+            nc.sync.dma_start(out=raw[name, e, first][:], in_=rows[:, :, first:last])
 
-        nc.sync.dma_start(tok_list[:], offs)
-        nc.sync.dma_start(out=xw[:], in_=x_words[0].rearrange("p t d -> p (t d)").bitcast(I32))
-        load_weight_half("w1", w1, 0, 0)
         nc.sync.dma_start(par_list[:], offs2)
+        nc.sync.dma_start(out=xw[:], in_=x_words[0].rearrange("p t d -> p (t d)").bitcast(I32))
         xs_rows = x_scales[0].bitcast(I32)
         for r in range(4):
             nc.sync.dma_start(out=xs[:].bitcast(I32)[r:P:32, :], in_=xs_rows[r:16:4, :])
-        load_weight_half("w1", w1, 0, 1)
         nc.sync.dma_start(
             out=wpw[:].bitcast(I32), in_=wp_words.rearrange("e s p b -> p (e s) b").bitcast(I32)
         )
+        load_weight("w1", w1, 0, 0, HALF)
+        load_weight("w1", w1, 0, HALF, H)
+        nc.sync.dma_start(tok_list[:], offs)
         wps_rows = wp_scales.rearrange("e s b i -> b (e s) i").bitcast(I32)
         for r in range(4):
             nc.sync.dma_start(out=wps[:].bitcast(I32)[r:P:32, :, :], in_=wps_rows[r:16:4, :, :])
-        load_weight_half("w1", w1, 1, 0)
-        load_weight_half("w1", w1, 1, 1)
-        load_weight_half("w2", w2, 0, 0)
-        load_weight_half("w2", w2, 0, 1)
+        load_weight("w2", w2, 0, 0, N)
         nc.sync.dma_start(out=gate_sb[:], in_=gate)
-        load_weight_half("w2", w2, 1, 0)
-        load_weight_half("w2", w2, 1, 1)
+        load_weight("w1", w1, 1, 0, HALF)
+        load_weight("w1", w1, 1, HALF, H)
+        load_weight("w2", w2, 1, 0, HALF)
+        load_weight("w2", w2, 1, HALF, N)
 
         gathered = {}
 
-        def gather(e):
-            cols = slice(e * LIST_COLS, (e + 1) * LIST_COLS)
-            for name, lst in (("tok", tok_list), ("par", par_list)):
-                words = tile([P, C], U32, "%s_words_%d" % (name, e))
-                nc.vector.tensor_copy(out=words[:], in_=xw[:].bitcast(U32).indirect(lst[:, cols]))
-                gathered[name, "words", e] = words
-            for name, lst in (("par", par_list), ("tok", tok_list)):
-                scales = tile([P, C], U8, "%s_scales_%d" % (name, e))
-                nc.vector.tensor_copy(out=scales[:], in_=xs[:].indirect(lst[:, cols]))
-                gathered[name, "scales", e] = scales
+        def gather(e, name, sort, tag=None):
+            lst = {"par": par_list, "tok": tok_list}[name][:, e * LIST_COLS : (e + 1) * LIST_COLS]
+            dtype, window = {"words": (U32, xw[:].bitcast(U32)), "scales": (U8, xs[:])}[sort]
+            gathered[name, sort, e] = tile([P, C], dtype, "%s_%s_%d" % (name, sort, e), tag)
+            nc.vector.tensor_copy(out=gathered[name, sort, e][:], in_=window.indirect(lst))
 
-        dealt = {}
+        wp_dealt_words = tile([P, E, 2 * H], U8, "wp_dealt_words")
+        wp_dealt_scales = {}
 
-        def deal_wp(e):
-            words = tile([P, 2 * H], U8, "wp_dealt_words_%d" % e)
-            nc.scalar.copy(
-                out=words[:].bitcast(U16).rearrange("p (t m) -> p m t", t=PACK),
-                in_=wpw[:, e, :].bitcast(U16).rearrange("p (m t) -> p m t", t=PACK),
-            )
-            scales = tile([P, H], U8, "wp_dealt_scales_%d" % e)
+        def deal_scales(e, tag=None):
+            wp_dealt_scales[e] = tile([P, H], U8, "wp_dealt_scales_%d" % e, tag)
             nc.vector.tensor_copy(
-                out=scales[:].rearrange("p (t m) -> p m t", t=PACK),
+                out=wp_dealt_scales[e][:].rearrange("p (t m) -> p m t", t=PACK),
                 in_=wps[:, e, :].rearrange("p (m t) -> p m t", t=PACK),
             )
-            dealt[e] = (words, scales)
 
         def round_on(engine, out, in_):
-            if engine == "gpsimd":
-                nc.gpsimd.tensor_scalar(out, in_, 1.0, 0.0, MULT, ADD)
-            elif engine == "scalar":
+            if engine == "scalar":
                 nc.scalar.copy(out=out, in_=in_)
             else:
                 nc.vector.tensor_copy(out=out, in_=in_)
@@ -114,141 +101,182 @@ def tile_moe_duo_relu_kernel(
         rounded = {}
         quantised = {}
 
-        def round_weight(name, e, engines):
-            for pair in range(2):
+        def round_weight(name, e, pair, first, engine, part=slice(None)):
+            if (name, e, pair) not in rounded:
                 rounded[name, e, pair] = tile([P, 2, P, PACK], BF16, "rounded_%s_%d_%d" % (name, e, pair))
-            for half in range(2):
-                src = raw[name, e, half][:].rearrange("p j (m t) -> p m j t", t=PACK)
-                for pair in range(2):
-                    dst = rounded[name, e, pair][:].rearrange("p t m j -> p m j t")
-                    round_on(
-                        engines[pair],
-                        dst[:, half * 64 : (half + 1) * 64, :, :],
-                        src[:, :, :, 2 * pair : 2 * pair + 2],
-                    )
+            src = raw[name, e, first][:].rearrange("p j (m t) -> p m j t", t=PACK)
+            dst = rounded[name, e, pair][:].rearrange("p t m j -> p m j t")
+            m0 = first // PACK
+            dst = dst[:, m0 : m0 + src.shape[1]]
+            round_on(engine, dst[:, part], src[:, part, :, 2 * pair : 2 * pair + 2])
 
-        def quantise_weight(name, e):
-            for pair in range(2):
-                codes = tile([P, 2 * P], U32, "codes_%s_%d_%d" % (name, e, pair))
-                scales = tile([P, 2 * P], U8, "scales_%s_%d_%d" % (name, e, pair))
-                nc.vector.quantize_mx(
-                    out=codes[:].bitcast(FP8X4),
-                    scales=scales[:],
-                    in_=rounded[name, e, pair][:].rearrange("p t m j -> p (t m j)"),
+        def quantise_weight(name, e, pair):
+            codes = tile([P, 2 * P], U32, "codes_%s_%d_%d" % (name, e, pair))
+            scales = tile([P, 2 * P], U8, "scales_%s_%d_%d" % (name, e, pair))
+            nc.vector.quantize_mx(
+                out=codes[:].bitcast(FP8X4),
+                scales=scales[:],
+                in_=rounded[name, e, pair][:].rearrange("p t m j -> p (t m j)"),
+            )
+            quantised[name, e, pair] = (codes, scales)
+
+        def stationary(name, e, t):
+            if name == "wp":
+                return (
+                    wp_dealt_words[:, e, 2 * P * t : 2 * P * (t + 1)].bitcast(FP4X4),
+                    wp_dealt_scales[e][:, P * t : P * (t + 1)],
                 )
-                quantised[name, e, pair] = (codes, scales)
+            codes, scales = quantised[name, e, t // 2]
+            cols = slice((t % 2) * P, (t % 2 + 1) * P)
+            return codes[:, cols].bitcast(FP8X4), scales[:, cols]
 
         h_banks = {}
-
-        def partner_products(e):
-            words, scales = dealt[e]
-            for s in range(2):
-                bank = ps.tile([P, PACK, P], F32, name="h_bank_%d_%d" % (e, s))
-                h_banks[e, s] = bank
-                slots = slice(s * P, (s + 1) * P)
-                for t in range(PACK):
-                    nc.tensor.matmul_mx(
-                        out=bank[:, t, :],
-                        lhsT=words[:, 2 * P * t : 2 * P * (t + 1)].bitcast(FP4X4),
-                        lhsT_scale=scales[:, P * t : P * (t + 1)],
-                        rhs=gathered["par", "words", e][:, slots].bitcast(FP8X4),
-                        rhs_scale=gathered["par", "scales", e][:, slots],
-                        start=(t == 0),
-                        stop=False,
-                    )
-
         hq = {}
 
-        def first_layer(e):
-            h_rounded = tile([P, C, PACK], BF16, "h_rounded_%d" % e)
+        def first_products(e, name, opens):
             for s in range(2):
-                bank = h_banks[e, s]
+                if opens:
+                    h_banks[e, s] = ps.tile([P, PACK, P], F32, name="h_bank_%d_%d" % (e, s))
                 slots = slice(s * P, (s + 1) * P)
                 for t in range(PACK):
-                    codes, scales = quantised["w1", e, t // 2]
-                    cols = slice((t % 2) * P, (t % 2 + 1) * P)
+                    codes, scales = stationary("wp" if name == "par" else "w1", e, t)
                     nc.tensor.matmul_mx(
-                        out=bank[:, t, :],
-                        lhsT=codes[:, cols].bitcast(FP8X4),
-                        lhsT_scale=scales[:, cols],
-                        rhs=gathered["tok", "words", e][:, slots].bitcast(FP8X4),
-                        rhs_scale=gathered["tok", "scales", e][:, slots],
-                        start=False,
-                        stop=(t == PACK - 1),
+                        out=h_banks[e, s][:, t, :],
+                        lhsT=codes,
+                        lhsT_scale=scales,
+                        rhs=gathered[name, "words", e][:, slots].bitcast(FP8X4),
+                        rhs_scale=gathered[name, "scales", e][:, slots],
+                        start=(opens and t == 0),
+                        stop=(not opens and t == PACK - 1),
                     )
-                nc.scalar.activation(
-                    out=h_rounded[:, slots, :], in_=bank[:].rearrange("p t n -> p n t"), func=RELU
-                )
+
+        def relu(e, engine, tag):
+            rounded["h", e] = tile([P, C, PACK], BF16, "h_rounded_%d" % e, tag)
+            for s in range(2):
+                out = rounded["h", e][:, s * P : (s + 1) * P, :]
+                sums = h_banks[e, s][:].rearrange("p t n -> p n t")
+                if engine == "scalar":
+                    nc.scalar.activation(out=out, in_=sums, func=RELU)
+                else:
+                    nc.vector.tensor_scalar_max(out, sums, 0.0)
+
+        def quantise_h(e):
             codes = tile([P, C], U32, "h_codes_%d" % e)
             scales = tile([P, C], U8, "h_scales_%d" % e)
             nc.vector.quantize_mx(
-                out=codes[:].bitcast(FP8X4), scales=scales[:], in_=h_rounded[:].rearrange("p n t -> p (n t)")
+                out=codes[:].bitcast(FP8X4), scales=scales[:], in_=rounded["h", e][:].rearrange("p n t -> p (n t)")
             )
             hq[e] = (codes, scales)
 
-        result = [tile([P, T], F32, "result_%d" % t) for t in range(PACK)]
+        result = {t: tile([P, T], F32, "result_%d" % t) for t in range(1, PACK - 1)}
+        gated = {}
+        y_banks = {}
 
-        def second_layer(e, scalar_tiles):
+        def second_products(e):
             h_codes, h_scales = hq[e]
-            cols = slice(e * LIST_COLS, (e + 1) * LIST_COLS)
-            gated = {}
-            for pair in range(2):
-                codes, scales = quantised["w2", e, pair]
-                bank = ps.tile([P, 2, C], F32, name="y_bank_%d_%d" % (e, pair))
-                for u in range(2):
-                    nc.tensor.matmul_mx(
-                        out=bank[:, u, :],
-                        lhsT=codes[:, u * P : (u + 1) * P].bitcast(FP8X4),
-                        lhsT_scale=scales[:, u * P : (u + 1) * P],
-                        rhs=h_codes[:].bitcast(FP8X4),
-                        rhs_scale=h_scales[:],
-                        start=True,
-                        stop=True,
-                    )
-                gated[pair] = tile([P, 2, C], F32, "gated_%d_%d" % (e, pair))
-                nc.vector.tensor_tensor(
-                    gated[pair][:],
-                    bank[:],
-                    gate_sb[:, e * C : (e + 1) * C].unsqueeze(1).to_broadcast([P, 2, C]),
-                    MULT,
-                )
             for t in range(PACK):
-                window = result[t][:].indirect(tok_list[:, cols])
-                values = gated[t // 2][:, t % 2, :]
-                if t < scalar_tiles:
-                    nc.scalar.activation(window, values, COPY)
-                else:
-                    nc.vector.tensor_copy(window, values)
+                if t % 2 == 0:
+                    y_banks[e, t // 2] = ps.tile([P, 2, C], F32, name="y_bank_%d_%d" % (e, t // 2))
+                codes, scales = stationary("w2", e, t)
+                nc.tensor.matmul_mx(
+                    out=y_banks[e, t // 2][:, t % 2, :],
+                    lhsT=codes,
+                    lhsT_scale=scales,
+                    rhs=h_codes[:].bitcast(FP8X4),
+                    rhs_scale=h_scales[:],
+                    start=True,
+                    stop=True,
+                )
 
-        gather(0)
-        gather(1)
-        deal_wp(0)
-        deal_wp(1)
-        round_weight("w1", 0, ("scalar", "scalar"))
-        round_weight("w1", 1, ("scalar", "scalar"))
-        partner_products(0)
-        partner_products(1)
-        quantise_weight("w1", 0)
-        first_layer(0)
-        quantise_weight("w1", 1)
-        first_layer(1)
-        round_weight("w2", 0, ("vector", "vector"))
-        quantise_weight("w2", 0)
-        second_layer(0, 4)
-        round_weight("w2", 1, ("vector", "vector"))
-        quantise_weight("w2", 1)
-        second_layer(1, 1)
+        def apply_gate(e, pair, tag=None):
+            gated[e, pair] = tile([P, 2, C], F32, "gated_%d_%d" % (e, pair), tag)
+            nc.vector.tensor_tensor(
+                gated[e, pair][:],
+                y_banks[e, pair][:],
+                gate_sb[:, e * C : (e + 1) * C].unsqueeze(1).to_broadcast([P, 2, C]),
+                MULT,
+            )
 
+        def scatter(engine, e, t):
+            window = result[t][:].indirect(tok_list[:, e * LIST_COLS : (e + 1) * LIST_COLS])
+            values = gated[e, t // 2][:, t % 2, :]
+            if engine == "scalar":
+                nc.scalar.activation(window, values, COPY)
+            else:
+                nc.vector.tensor_copy(window, values)
+
+        for e, name in ((0, "par"), (1, "par"), (0, "tok")):
+            gather(e, name, "words")
+            gather(e, name, "scales")
+        for e in range(E):
+            nc.scalar.copy(
+                out=wp_dealt_words[:, e, :].bitcast(U16).rearrange("p (t m) -> p t m", t=PACK),
+                in_=wpw[:, e, :].bitcast(U16).rearrange("p (m t) -> p t m", t=PACK),
+            )
+        deal_scales(0)
+        for first in (0, HALF):
+            for pair in range(2):
+                round_weight("w1", 0, pair, first, "scalar")
+        quantise_weight("w1", 0, 0)
+        quantise_weight("w1", 0, 1)
+        first_products(0, "tok", True)
+        first_products(0, "par", False)
+        deal_scales(1, "rounded_w1_0_1")
+        round_weight("w2", 0, 0, 0, "scalar", slice(0, 64))
+        round_weight("w2", 0, 1, 0, "vector")
+        round_weight("w2", 0, 0, 0, "vector", slice(64, P))
+        relu(0, "scalar", "raw_w2_0_0")
+        quantise_weight("w2", 0, 1)
+        quantise_weight("w2", 0, 0)
+        gather(1, "tok", "words", "rounded_w2_0_0")
+        quantise_h(0)
+        gather(1, "tok", "scales", "raw_w2_0_0")
+        second_products(0)
+        first_products(1, "par", True)
+        for pair in range(2):
+            round_weight("w1", 1, pair, 0, "scalar")
+            round_weight("w1", 1, pair, HALF, "vector")
+        apply_gate(0, 0, "raw_w1_1_256")
+        quantise_weight("w1", 1, 0)
+        quantise_weight("w1", 1, 1)
+        apply_gate(0, 1)
+        result[0] = tile([P, T], F32, "result_0", "raw_w1_1_0")
+        for t in range(PACK - 1):
+            scatter("scalar", 0, t)
+        first_products(1, "tok", False)
+        for pair in range(2):
+            round_weight("w2", 1, pair, 0, "vector")
+        relu(1, "vector", "raw_w2_1_0")
+        quantise_h(1)
+        for pair in range(2):
+            round_weight("w2", 1, pair, HALF, "vector")
+        quantise_weight("w2", 1, 0)
+        quantise_weight("w2", 1, 1)
+        second_products(1)
+        result[3] = tile([P, T], F32, "result_3", "rounded_w2_1_1")
+        scatter("vector", 0, 3)
+        apply_gate(1, 0)
+        apply_gate(1, 1)
         out_rows = out_0.rearrange("(p t) c -> p t c", t=PACK)
-        planes = tile([P, PACK, T], BF16, "planes")
-        for t, engine in ((0, "scalar"), (1, "scalar"), (2, "scalar"), (3, "vector")):
-            nc.sync.dma_start(out=out_rows[:, t, :], in_=result[t][:])
-            round_on(engine, planes[:, t, :], result[t][:])
+        pairs = tile([P, 2, T, 2], BF16, "pairs")
+        for v in range(2):
+            for u, engine in ((0, "scalar"), (1, "vector")):
+                t = 2 * u + v
+                scatter(engine, 1, t)
+                nc.sync.dma_start(out=out_rows[:, t, :], in_=result[t][:])
+                round_on(engine, pairs[:, u, :, v], result[t][:])
         woven = tile([P, T, PACK], BF16, "woven")
-        src = planes[:].rearrange("p t (c i) -> p c t i", i=4)
-        dst = woven[:].rearrange("p (c i) t -> p c t i", i=4)
-        nc.vector.tensor_copy(out=dst[:, :96], in_=src[:, :96])
-        nc.scalar.copy(out=dst[:, 96:], in_=src[:, 96:])
+        src = pairs[:].rearrange("p u c v -> p u (c v)")
+        dst = woven[:].rearrange("p c t -> p (c t)")
+        split = 88
+        nc.vector.tensor_copy(
+            out=dst.bitcast(I32).rearrange("p (c i u) -> p c u i", i=4, u=2)[:, :split],
+            in_=src.bitcast(I32).rearrange("p u (c i) -> p c u i", i=4)[:, :split],
+        )
+        nc.scalar.copy(
+            out=dst.bitcast(U32).rearrange("p (c i u) -> p c u i", i=4, u=2)[:, split:],
+            in_=src.bitcast(U32).rearrange("p u (c i) -> p c u i", i=4)[:, split:],
+        )
         out_codes = tile([P, T], I32, "out_codes")
         out_scales = tile([P, T], U8, "out_scales")
         nc.vector.quantize_mx(

from contextlib import ExitStack

import concourse.mybir as mybir

K, T, E, C, H, N = 512, 512, 2, 256, 512, 512
FLOPS = 2 * E * C * (2 * K * H + H * N)

F32 = mybir.dt.float32
BF16 = mybir.dt.bfloat16
I32 = mybir.dt.int32
U32 = mybir.dt.uint32
U16 = mybir.dt.uint16
U8 = mybir.dt.uint8
FP8X4 = mybir.dt.float8_e4m3fn_x4
FP4X4 = mybir.dt.float4_e2m1fn_x4
MULT = mybir.AluOpType.mult
ADD = mybir.AluOpType.add
RELU = mybir.ActivationFunctionType.Relu
COPY = mybir.ActivationFunctionType.Copy

P = 128
PACK = 4
HALF = 256
LIST_COLS = C // 16


def tile_moe_duo_relu_kernel(
    tc, x_words, x_scales, w1, wp_words, wp_scales, w2, gate, offs, offs2, out_0, out_1, out_2
):
    nc = tc.nc
    with ExitStack() as ctx:
        sb = ctx.enter_context(tc.tile_pool(name="sb", bufs=1))
        ps = ctx.enter_context(tc.psum_pool(name="ps", bufs=1))

        def tile(shape, dtype, name, tag=None):
            return sb.tile(shape, dtype, name=name, tag=tag or name, align_bytes=64)

        tok_list = sb.tile([P, T // 16], U16, name="tok_list")
        par_list = sb.tile([P, T // 16], U16, name="par_list")
        xw = tile([P, T], I32, "xw")
        xs = tile([P, T], U8, "xs")
        wpw = tile([P, E, 2 * H], U8, "wpw")
        wps = tile([P, E, H], U8, "wps")
        gate_sb = tile([P, E * C], F32, "gate_sb")

        nc.gpsimd.memset(xs[:].bitcast(I32), 0)
        nc.gpsimd.memset(wps[:].rearrange("p e i -> p (e i)").bitcast(I32), 0)

        raw = {}

        def load_weight(name, w, e, first, last):
            raw[name, e, first] = tile([P, PACK, last - first], F32, "raw_%s_%d_%d" % (name, e, first))
            rows = w[e].rearrange("(p j) c -> p j c", j=PACK)
            nc.sync.dma_start(out=raw[name, e, first][:], in_=rows[:, :, first:last])

        nc.sync.dma_start(par_list[:], offs2)
        nc.sync.dma_start(out=xw[:], in_=x_words[0].rearrange("p t d -> p (t d)").bitcast(I32))
        xs_rows = x_scales[0].bitcast(I32)
        for r in range(4):
            nc.sync.dma_start(out=xs[:].bitcast(I32)[r:P:32, :], in_=xs_rows[r:16:4, :])
        nc.sync.dma_start(
            out=wpw[:].bitcast(I32), in_=wp_words.rearrange("e s p b -> p (e s) b").bitcast(I32)
        )
        load_weight("w1", w1, 0, 0, HALF)
        load_weight("w1", w1, 0, HALF, H)
        nc.sync.dma_start(tok_list[:], offs)
        wps_rows = wp_scales.rearrange("e s b i -> b (e s) i").bitcast(I32)
        for r in range(4):
            nc.sync.dma_start(out=wps[:].bitcast(I32)[r:P:32, :, :], in_=wps_rows[r:16:4, :, :])
        load_weight("w2", w2, 0, 0, N)
        nc.sync.dma_start(out=gate_sb[:], in_=gate)
        load_weight("w1", w1, 1, 0, HALF)
        load_weight("w1", w1, 1, HALF, H)
        load_weight("w2", w2, 1, 0, HALF)
        load_weight("w2", w2, 1, HALF, N)

        gathered = {}

        def gather(e, name, sort, tag=None):
            lst = {"par": par_list, "tok": tok_list}[name][:, e * LIST_COLS : (e + 1) * LIST_COLS]
            dtype, window = {"words": (U32, xw[:].bitcast(U32)), "scales": (U8, xs[:])}[sort]
            gathered[name, sort, e] = tile([P, C], dtype, "%s_%s_%d" % (name, sort, e), tag)
            nc.vector.tensor_copy(out=gathered[name, sort, e][:], in_=window.indirect(lst))

        wp_dealt_words = tile([P, E, 2 * H], U8, "wp_dealt_words")
        wp_dealt_scales = {}

        def deal_scales(e, tag=None):
            wp_dealt_scales[e] = tile([P, H], U8, "wp_dealt_scales_%d" % e, tag)
            nc.vector.tensor_copy(
                out=wp_dealt_scales[e][:].rearrange("p (t m) -> p m t", t=PACK),
                in_=wps[:, e, :].rearrange("p (m t) -> p m t", t=PACK),
            )

        def round_on(engine, out, in_):
            if engine == "scalar":
                nc.scalar.copy(out=out, in_=in_)
            else:
                nc.vector.tensor_copy(out=out, in_=in_)

        rounded = {}
        quantised = {}

        def round_weight(name, e, pair, first, engine, part=slice(None)):
            if (name, e, pair) not in rounded:
                rounded[name, e, pair] = tile([P, 2, P, PACK], BF16, "rounded_%s_%d_%d" % (name, e, pair))
            src = raw[name, e, first][:].rearrange("p j (m t) -> p m j t", t=PACK)
            dst = rounded[name, e, pair][:].rearrange("p t m j -> p m j t")
            m0 = first // PACK
            dst = dst[:, m0 : m0 + src.shape[1]]
            round_on(engine, dst[:, part], src[:, part, :, 2 * pair : 2 * pair + 2])

        def quantise_weight(name, e, pair):
            codes = tile([P, 2 * P], U32, "codes_%s_%d_%d" % (name, e, pair))
            scales = tile([P, 2 * P], U8, "scales_%s_%d_%d" % (name, e, pair))
            nc.vector.quantize_mx(
                out=codes[:].bitcast(FP8X4),
                scales=scales[:],
                in_=rounded[name, e, pair][:].rearrange("p t m j -> p (t m j)"),
            )
            quantised[name, e, pair] = (codes, scales)

        def stationary(name, e, t):
            if name == "wp":
                return (
                    wp_dealt_words[:, e, 2 * P * t : 2 * P * (t + 1)].bitcast(FP4X4),
                    wp_dealt_scales[e][:, P * t : P * (t + 1)],
                )
            codes, scales = quantised[name, e, t // 2]
            cols = slice((t % 2) * P, (t % 2 + 1) * P)
            return codes[:, cols].bitcast(FP8X4), scales[:, cols]

        h_banks = {}
        hq = {}

        def first_products(e, name, opens):
            for s in range(2):
                if opens:
                    h_banks[e, s] = ps.tile([P, PACK, P], F32, name="h_bank_%d_%d" % (e, s))
                slots = slice(s * P, (s + 1) * P)
                for t in range(PACK):
                    codes, scales = stationary("wp" if name == "par" else "w1", e, t)
                    nc.tensor.matmul_mx(
                        out=h_banks[e, s][:, t, :],
                        lhsT=codes,
                        lhsT_scale=scales,
                        rhs=gathered[name, "words", e][:, slots].bitcast(FP8X4),
                        rhs_scale=gathered[name, "scales", e][:, slots],
                        start=(opens and t == 0),
                        stop=(not opens and t == PACK - 1),
                    )

        def relu(e, engine, tag):
            rounded["h", e] = tile([P, C, PACK], BF16, "h_rounded_%d" % e, tag)
            for s in range(2):
                out = rounded["h", e][:, s * P : (s + 1) * P, :]
                sums = h_banks[e, s][:].rearrange("p t n -> p n t")
                if engine == "scalar":
                    nc.scalar.activation(out=out, in_=sums, func=RELU)
                else:
                    nc.vector.tensor_scalar_max(out, sums, 0.0)

        def quantise_h(e):
            codes = tile([P, C], U32, "h_codes_%d" % e)
            scales = tile([P, C], U8, "h_scales_%d" % e)
            nc.vector.quantize_mx(
                out=codes[:].bitcast(FP8X4), scales=scales[:], in_=rounded["h", e][:].rearrange("p n t -> p (n t)")
            )
            hq[e] = (codes, scales)

        result = {t: tile([P, T], F32, "result_%d" % t) for t in range(1, PACK - 1)}
        gated = {}
        y_banks = {}

        def second_products(e):
            h_codes, h_scales = hq[e]
            for t in range(PACK):
                if t % 2 == 0:
                    y_banks[e, t // 2] = ps.tile([P, 2, C], F32, name="y_bank_%d_%d" % (e, t // 2))
                codes, scales = stationary("w2", e, t)
                nc.tensor.matmul_mx(
                    out=y_banks[e, t // 2][:, t % 2, :],
                    lhsT=codes,
                    lhsT_scale=scales,
                    rhs=h_codes[:].bitcast(FP8X4),
                    rhs_scale=h_scales[:],
                    start=True,
                    stop=True,
                )

        def apply_gate(e, pair, tag=None):
            gated[e, pair] = tile([P, 2, C], F32, "gated_%d_%d" % (e, pair), tag)
            nc.vector.tensor_tensor(
                gated[e, pair][:],
                y_banks[e, pair][:],
                gate_sb[:, e * C : (e + 1) * C].unsqueeze(1).to_broadcast([P, 2, C]),
                MULT,
            )

        def scatter(engine, e, t):
            window = result[t][:].indirect(tok_list[:, e * LIST_COLS : (e + 1) * LIST_COLS])
            values = gated[e, t // 2][:, t % 2, :]
            if engine == "scalar":
                nc.scalar.activation(window, values, COPY)
            else:
                nc.vector.tensor_copy(window, values)

        for e, name in ((0, "par"), (1, "par"), (0, "tok")):
            gather(e, name, "words")
            gather(e, name, "scales")
        for e in range(E):
            nc.scalar.copy(
                out=wp_dealt_words[:, e, :].bitcast(U16).rearrange("p (t m) -> p t m", t=PACK),
                in_=wpw[:, e, :].bitcast(U16).rearrange("p (m t) -> p t m", t=PACK),
            )
        deal_scales(0)
        for first in (0, HALF):
            for pair in range(2):
                round_weight("w1", 0, pair, first, "scalar")
        quantise_weight("w1", 0, 0)
        quantise_weight("w1", 0, 1)
        first_products(0, "tok", True)
        first_products(0, "par", False)
        deal_scales(1, "rounded_w1_0_1")
        round_weight("w2", 0, 0, 0, "scalar", slice(0, 64))
        round_weight("w2", 0, 1, 0, "vector")
        round_weight("w2", 0, 0, 0, "vector", slice(64, P))
        relu(0, "scalar", "raw_w2_0_0")
        quantise_weight("w2", 0, 1)
        quantise_weight("w2", 0, 0)
        gather(1, "tok", "words", "rounded_w2_0_0")
        quantise_h(0)
        gather(1, "tok", "scales", "raw_w2_0_0")
        second_products(0)
        first_products(1, "par", True)
        for pair in range(2):
            round_weight("w1", 1, pair, 0, "scalar")
            round_weight("w1", 1, pair, HALF, "vector")
        apply_gate(0, 0, "raw_w1_1_256")
        quantise_weight("w1", 1, 0)
        quantise_weight("w1", 1, 1)
        apply_gate(0, 1)
        result[0] = tile([P, T], F32, "result_0", "raw_w1_1_0")
        for t in range(PACK - 1):
            scatter("scalar", 0, t)
        first_products(1, "tok", False)
        for pair in range(2):
            round_weight("w2", 1, pair, 0, "vector")
        relu(1, "vector", "raw_w2_1_0")
        quantise_h(1)
        for pair in range(2):
            round_weight("w2", 1, pair, HALF, "vector")
        quantise_weight("w2", 1, 0)
        quantise_weight("w2", 1, 1)
        second_products(1)
        result[3] = tile([P, T], F32, "result_3", "rounded_w2_1_1")
        scatter("vector", 0, 3)
        apply_gate(1, 0)
        apply_gate(1, 1)
        out_rows = out_0.rearrange("(p t) c -> p t c", t=PACK)
        pairs = tile([P, 2, T, 2], BF16, "pairs")
        for v in range(2):
            for u, engine in ((0, "scalar"), (1, "vector")):
                t = 2 * u + v
                scatter(engine, 1, t)
                nc.sync.dma_start(out=out_rows[:, t, :], in_=result[t][:])
                round_on(engine, pairs[:, u, :, v], result[t][:])
        woven = tile([P, T, PACK], BF16, "woven")
        src = pairs[:].rearrange("p u c v -> p u (c v)")
        dst = woven[:].rearrange("p c t -> p (c t)")
        split = 88
        nc.vector.tensor_copy(
            out=dst.bitcast(I32).rearrange("p (c i u) -> p c u i", i=4, u=2)[:, :split],
            in_=src.bitcast(I32).rearrange("p u (c i) -> p c u i", i=4)[:, :split],
        )
        nc.scalar.copy(
            out=dst.bitcast(U32).rearrange("p (c i u) -> p c u i", i=4, u=2)[:, split:],
            in_=src.bitcast(U32).rearrange("p u (c i) -> p c u i", i=4)[:, split:],
        )
        out_codes = tile([P, T], I32, "out_codes")
        out_scales = tile([P, T], U8, "out_scales")
        nc.vector.quantize_mx(
            out=out_codes[:].bitcast(FP8X4), scales=out_scales[:], in_=woven[:].rearrange("p c t -> p (c t)")
        )
        nc.sync.dma_start(out=out_1[0].rearrange("p t d -> p (t d)").bitcast(I32), in_=out_codes[:])
        scale_rows = out_2[0].bitcast(I32)
        for q in range(4):
            queue = nc.scalar if q % 2 else nc.sync
            queue.dma_start(
                out=scale_rows[4 * q : 4 * q + 4, :], in_=out_scales[:].bitcast(I32)[32 * q : 32 * q + 4, :]
            )
